import numpy as np
import ml_dtypes


def mxq(x, axis, fmt="e4m3"):
    dtype, down = {"e4m3": (ml_dtypes.float8_e4m3fn, 7), "e5m2": (ml_dtypes.float8_e5m2, 14)}[fmt]
    v = np.moveaxis(np.asarray(x, np.float32).astype(ml_dtypes.bfloat16).astype(np.float64), axis, -1)
    blocks = v.reshape(v.shape[:-1] + (-1, 32))
    amax = np.abs(blocks).max(-1, keepdims=True)
    byte = np.maximum(np.where(amax > 0, np.frexp(amax)[1] - 1 + 127, 0) - down, 1)
    scale = np.exp2(byte - 127.0)
    codes = (blocks / scale).astype(np.float32).astype(dtype).astype(np.float64)
    return np.moveaxis((codes * scale).reshape(v.shape), -1, axis)


WIDE = False


def mx_kscale(k):
    if not WIDE:
        return np.ones(k)
    levels = np.array([10, -10, 5, -5, 0])
    if k % 512:
        return np.exp2(np.random.permutation(np.resize(levels, k // 32))).repeat(32)
    a = np.empty((k // 512, 16))
    for p in range(k // 512):
        a[p, :8] = np.random.permutation(np.resize(levels, 8))
        for g in range(8):
            far = levels[np.abs(levels - a[p, g]) >= 10]
            a[p, g + 8] = far[np.random.randint(len(far))]
    return np.exp2(a.ravel()).repeat(32)


def f64(x):
    return np.asarray(x).astype(np.float64)


def striped(idx):
    return np.tile(np.asarray(idx).reshape(-1, 16).T, (8, 1)).astype(np.uint16)


def unstriped(offs):
    return offs[:16].T.reshape(-1).astype(np.int64)


E2M1 = np.array([0.0, 0.5, 1.0, 1.5, 2.0, 3.0, 4.0, 6.0, -0.0, -0.5, -1.0, -1.5, -2.0, -3.0, -4.0, -6.0])


def pack_weight(w, fmt):
    k, n = w.shape
    w = f64(np.asarray(w, np.float32).astype(ml_dtypes.bfloat16)).reshape(k // 32, 32, n)
    amax = np.abs(w).max(1)
    if fmt == "e4m3":
        byte = np.frexp(amax)[1] - 1 + 127 - 7
    else:
        mant, ex = np.frexp(amax / 6.0)
        byte = np.where(mant > 0.5, ex, ex - 1) + 127
    byte = np.clip(np.where(amax > 0, byte, 1), 1, 254)
    scaled = (w * np.exp2(127.0 - byte)[:, None, :]).reshape(k, n).astype(np.float32)
    by_word = np.ascontiguousarray(scaled.reshape(k // 512, 128, 4, n).transpose(0, 1, 3, 2))
    if fmt == "e4m3":
        words = by_word.astype(ml_dtypes.float8_e4m3fn).view(np.uint8)
    else:
        c = by_word.astype(ml_dtypes.float4_e2m1fn).view(np.uint8) & 0xF
        words = (c[..., 0::2] | (c[..., 1::2] << 4)).reshape(k // 512, 128, 2 * n)
    return np.ascontiguousarray(words), np.ascontiguousarray(byte.astype(np.uint8).reshape(k // 512, 16, n))


def unpack_weight(words, scales, fmt):
    g, _, n = scales.shape
    words = np.ascontiguousarray(words).reshape(g, 128, n, -1)
    if fmt == "e4m3":
        vals = words.view(ml_dtypes.float8_e4m3fn).astype(np.float64)
    else:
        nib = np.empty((g, 128, n, 4), np.uint8)
        nib[..., 0::2] = words & 0xF
        nib[..., 1::2] = words >> 4
        vals = E2M1[nib]
    vals = vals * np.repeat(np.exp2(scales.astype(np.float64) - 127.0), 8, axis=1)[..., None]
    return vals.transpose(0, 1, 3, 2).reshape(g * 512, n)


D, T, I, J, U, Z, E, M, C = 512, 2048, 512, 256, 1024, 1024, 512, 1024, 512


def setup_inputs():
    n = np.random.standard_normal
    idx = np.random.permutation(T)[:I]
    idx2 = np.random.permutation(U)[:J]
    idx3 = np.random.permutation(Z)[:J]
    idx4 = np.random.permutation(M)[:J]
    fd = mx_kscale(D)
    fi = mx_kscale(I)
    fc = mx_kscale(C)
    ti = np.ones(T)
    ti[idx] = fi
    keysp = pack_weight(n((D, T)) / fd[:, None], "e4m3")
    return {
        "keys_words": keysp[0],
        "keys_scales": keysp[1],
        "notes": (n((D, U)) * 1.0 / np.sqrt(D) * fd[:, None]).astype(np.float32),
        "given": (np.random.uniform(0.3, 1.7, (I, Z))).astype(np.float32),
        "rowf": (np.random.uniform(0.02, 0.08, (I, 1)) * fi[:, None]).astype(np.float32),
        "vals": (n((E, T)) / ti).astype(np.float32),
        "wm": (n((C, E)) * 1.0 / np.sqrt(C) * fc[:, None]).astype(np.float32),
        "mstore": (n((C, M)) / fc[:, None]).astype(np.float32),
        "offs": striped(idx),
        "offs2": striped(idx2),
        "offs3": striped(idx3),
        "offs4": striped(idx4),
    }


def reference(keys_words, keys_scales, notes, given, rowf, vals, wm, mstore, offs, offs2, offs3, offs4):
    idx = unstriped(offs)
    idx2 = unstriped(offs2)
    idx3 = unstriped(offs3)
    idx4 = unstriped(offs4)
    keysu = unpack_weight(keys_words, keys_scales, "e4m3")
    keysidxg = keysu[:, idx]
    notesidx2q = mxq(f64(notes)[:, idx2], 0, "e4m3")
    g1 = keysidxg.T @ notesidx2q
    g0 = g1 * f64(given)[:, idx3]
    gr1 = g0 * f64(rowf)
    vt1 = f64(vals)[:, idx].T
    vt1q = mxq(vt1, 0, "e4m3")
    gr1q = mxq(gr1, 0, "e4m3")
    o = vt1q.T @ gr1q
    wmq = mxq(f64(wm), 0, "e4m3")
    mstoreq = mxq(f64(mstore), 0, "e4m3")
    me = wmq.T @ mstoreq
    y = o * me[:, idx4]
    return y

@@ -1,0 +1,195 @@
+from contextlib import ExitStack
+
+import concourse.mybir as mybir
+from concourse.masks import make_identity
+
+D, T, I, J, U, Z, E, M, C = 512, 2048, 512, 256, 1024, 1024, 512, 1024, 512
+FLOPS = 2 * (D * I * J + I * E * J + C * E * M)
+
+F32 = mybir.dt.float32
+BF16 = mybir.dt.bfloat16
+I32 = mybir.dt.int32
+U32 = mybir.dt.uint32
+U16 = mybir.dt.uint16
+U8 = mybir.dt.uint8
+FP8X4 = mybir.dt.float8_e4m3fn_x4
+MULT = mybir.AluOpType.mult
+COPY = mybir.ActivationFunctionType.Copy
+
+P = 128
+PACK = 4
+BANK = 512
+E_TILES = E // P
+
+
+def interleave(copy, dst, src):
+    copy(out=dst.rearrange("p (c i) t -> p c t i", i=4), in_=src.rearrange("p t (c i) -> p c t i", i=4))
+
+
+def quantize(nc, pool, name, grouped):
+    width = grouped.shape[1]
+    codes = pool.tile([P, width], U32, name=name + "_codes", align_bytes=64)
+    scales = pool.tile([P, width], U8, name=name + "_scales", align_bytes=64)
+    nc.vector.quantize_mx(out=codes[:].bitcast(FP8X4), scales=scales[:], in_=grouped.rearrange("p c t -> p (c t)"))
+    return codes, scales
+
+
+def product(nc, out, lhs, lhs_cols, rhs):
+    nc.tensor.matmul_mx(
+        out=out,
+        lhsT=lhs[0][:, lhs_cols].bitcast(FP8X4),
+        lhsT_scale=lhs[1][:, lhs_cols],
+        rhs=rhs[0][:].bitcast(FP8X4),
+        rhs_scale=rhs[1][:],
+        start=True,
+        stop=True,
+    )
+
+
+def tile_attend_tab_timestable_gains_kernel(
+    tc, keys_words, keys_scales, notes, given, rowf, vals, wm, mstore, offs, offs2, offs3, offs4, out
+):
+    nc = tc.nc
+    with ExitStack() as ctx:
+        lists = ctx.enter_context(tc.tile_pool(name="lists", bufs=1))
+        sb = ctx.enter_context(tc.tile_pool(name="sb", bufs=1))
+        wide = ctx.enter_context(tc.psum_pool(name="wide", bufs=4))
+        narrow = ctx.enter_context(tc.psum_pool(name="narrow", bufs=2))
+
+        def load_list(name, src):
+            tile = lists.tile(list(src.shape), U16, name=name)
+            nc.sync.dma_start(tile[:], src)
+            return tile
+
+        def load_pairs(name, src):
+            width = src.shape[1]
+            rows = src.rearrange("(p t) w -> p t w", t=PACK)
+            planes = []
+            for h in range(2):
+                tile = sb.tile([P, 2, width], F32, name="%s%d" % (name, h))
+                nc.sync.dma_start(out=tile[:], in_=rows[:, 2 * h : 2 * h + 2, :])
+                planes += [tile[:, 0, :], tile[:, 1, :]]
+            return planes
+
+        wm_raw = sb.tile([P, PACK, E], F32, name="wm_raw")
+        nc.sync.dma_start(out=wm_raw[:], in_=wm.rearrange("(p t) e -> p t e", t=PACK))
+        ms_raw = sb.tile([P, PACK, M], F32, name="ms_raw")
+        nc.sync.dma_start(out=ms_raw[:], in_=mstore.rearrange("(p t) m -> p t m", t=PACK))
+        idx = load_list("idx", offs)
+        key_words = sb.tile([P, T], I32, name="key_words")
+        nc.sync.dma_start(out=key_words[:], in_=keys_words[0].rearrange("p n t -> p (n t)").bitcast(I32))
+        idx2 = load_list("idx2", offs2)
+        note_planes = load_pairs("notes", notes)
+        idx4 = load_list("idx4", offs4)
+        idx3 = load_list("idx3", offs3)
+        given_planes = load_pairs("given", given)
+        val_rows = []
+        for e in range(E_TILES):
+            tile = sb.tile([P, T], F32, name="vals%d" % e, tag="vals%d" % e)
+            nc.sync.dma_start(out=tile[:], in_=vals[e * P : (e + 1) * P, :])
+            val_rows.append(tile)
+
+        ident = sb.tile([P, P], F32, name="ident")
+        make_identity(nc, ident[:])
+        key_bytes = sb.tile([P, T], U8, name="key_bytes")
+        nc.vector.memset(key_bytes[:].bitcast(I32), 0)
+        for q in range(4):
+            nc.gpsimd.dma_start(
+                out=key_bytes[32 * q : 32 * q + 4, :].bitcast(I32),
+                in_=keys_scales[0, 4 * q : 4 * q + 4, :].bitcast(I32),
+            )
+        row_factor = sb.tile([P, PACK], F32, name="row_factor")
+        nc.gpsimd.dma_start(out=row_factor[:], in_=rowf.rearrange("(p t) o -> p (t o)", t=PACK))
+
+        wm_grouped = sb.tile([P, E, PACK], BF16, name="wm_grouped", align_bytes=64)
+        interleave(nc.vector.tensor_copy, wm_grouped[:], wm_raw[:])
+        wm_q = quantize(nc, sb, "wm", wm_grouped[:])
+        ms_grouped = []
+        for h, copy in enumerate((nc.vector.tensor_copy, nc.scalar.copy)):
+            grouped = sb.tile([P, BANK, PACK], BF16, name="ms_grouped%d" % h, align_bytes=64)
+            interleave(copy, grouped[:], ms_raw[:, :, h * BANK : (h + 1) * BANK])
+            ms_grouped.append(grouped)
+        me = [sb.tile([P, M], F32, name="me%d" % e) for e in range(E_TILES)]
+        for h in range(2):
+            ms_q = quantize(nc, sb, "ms%d" % h, ms_grouped[h][:])
+            for e in range(E_TILES):
+                bank = wide.tile([P, BANK], F32, name="bank")
+                product(nc, bank[:], wm_q, slice(e * P, (e + 1) * P), ms_q)
+                nc.scalar.copy(out=me[e][:, h * BANK : (h + 1) * BANK], in_=bank[:])
+
+        key_codes = sb.tile([P, I], U32, name="key_codes", align_bytes=64)
+        key_scales = sb.tile([P, I], U8, name="key_scales", align_bytes=64)
+        nc.vector.tensor_copy(
+            out=key_scales[:].rearrange("p (t s) -> p s t", t=PACK), in_=key_bytes[:].indirect(idx[:])
+        )
+        nc.vector.tensor_copy(
+            out=key_codes[:].rearrange("p (t s) -> p s t", t=PACK), in_=key_words[:].bitcast(U32).indirect(idx[:])
+        )
+
+        note_cols = sb.tile([P, PACK, J], F32, name="note_cols")
+        for t in range(PACK):
+            nc.vector.tensor_copy(out=note_cols[:, t, :], in_=note_planes[t].indirect(idx2[:]))
+        note_grouped = sb.tile([P, J, PACK], BF16, name="note_grouped", align_bytes=64)
+        interleave(nc.vector.tensor_copy, note_grouped[:], note_cols[:])
+        note_q = quantize(nc, sb, "notes", note_grouped[:])
+
+        me_cols = []
+        for e in range(E_TILES):
+            cols = sb.tile([P, J], F32, name="me_cols%d" % e)
+            nc.scalar.activation(cols[:], me[e][:].indirect(idx4[:]), COPY)
+            me_cols.append(cols)
+
+        table = sb.tile([P, PACK, J], BF16, name="table")
+        for h in range(2):
+            bank = wide.tile([P, BANK], F32, name="bank")
+            for t in (2 * h, 2 * h + 1):
+                product(nc, bank[:, (t % 2) * J : (t % 2 + 1) * J], (key_codes, key_scales), slice(t * P, (t + 1) * P), note_q)
+            for t in (2 * h, 2 * h + 1):
+                given_cols = sb.tile([P, J], F32, name="given_cols%d" % t)
+                nc.scalar.activation(given_cols[:], given_planes[t].indirect(idx3[:]), COPY)
+                nc.vector.scalar_tensor_tensor(
+                    out=table[:, t, :],
+                    in0=given_cols[:],
+                    scalar=row_factor[:, t : t + 1],
+                    in1=bank[:, (t % 2) * J : (t % 2 + 1) * J],
+                    op0=MULT,
+                    op1=MULT,
+                )
+        table_grouped = sb.tile([P, J, PACK], BF16, name="table_grouped", align_bytes=64)
+        interleave(nc.vector.tensor_copy, table_grouped[:], table[:])
+        table_q = quantize(nc, sb, "table", table_grouped[:])
+
+        half = 288
+
+        def turn(e):
+            val_cols = sb.tile([P, I], BF16, name="val_cols%d" % e)
+            nc.vector.tensor_copy(out=val_cols[:, :half], in_=val_rows[e][:].indirect(idx[:, : half // 16]))
+            nc.scalar.activation(val_cols[:, half:], val_rows[e][:].indirect(idx[:, half // 16 :]), COPY)
+            words = val_cols[:].bitcast(F32)
+            turned = narrow.tile([P, 2, P], F32, name="turned")
+            for u in range(2):
+                nc.tensor.transpose(turned[:, u, :], words[:, u : I // 2 : 2], ident[:])
+            val_grouped = sb.tile([P, P, PACK], BF16, name="val_grouped%d" % e, align_bytes=64)
+            nc.scalar.copy(
+                out=val_grouped[:].rearrange("p c t -> p (c t)").bitcast(F32).rearrange("p (c u) -> p c u", u=2),
+                in_=turned[:].rearrange("p u c -> p c u"),
+            )
+            return val_grouped
+
+        def multiply(e, val_grouped):
+            val_q = quantize(nc, sb, "vals%d" % e, val_grouped[:])
+            sums = narrow.tile([P, J], F32, name="sums")
+            product(nc, sums[:], val_q, slice(0, P), table_q)
+            return sums
+
+        def finish(e, sums):
+            result = sb.tile([P, J], F32, name="result%d" % e, tag="vals%d" % (e + 1))
+            nc.vector.tensor_tensor(out=result[:], in0=sums[:], in1=me_cols[e][:], op=MULT)
+            nc.sync.dma_start(out=out[e * P : (e + 1) * P, :], in_=result[:])
+
+        sums = multiply(0, turn(0))
+        for e in range(1, E_TILES):
+            val_grouped = turn(e)
+            finish(e - 1, sums)
+            sums = multiply(e, val_grouped)
+        finish(E_TILES - 1, sums)

@@ -26,9 +26,9 @@ def interleave(copy, dst, src):
     copy(out=dst.rearrange("p (c i) t -> p c t i", i=4), in_=src.rearrange("p t (c i) -> p c t i", i=4))
 
 
-def quantize(nc, pool, name, grouped):
+def quantize(nc, pool, name, grouped, tag=None):
     width = grouped.shape[1]
-    codes = pool.tile([P, width], U32, name=name + "_codes", align_bytes=64)
+    codes = pool.tile([P, width], U32, name=name + "_codes", tag=tag or name + "_codes", align_bytes=64)
     scales = pool.tile([P, width], U8, name=name + "_scales", align_bytes=64)
     nc.vector.quantize_mx(out=codes[:].bitcast(FP8X4), scales=scales[:], in_=grouped.rearrange("p c t -> p (c t)"))
     return codes, scales
@@ -75,17 +75,17 @@ def tile_attend_tab_timestable_gains_kernel(
         nc.sync.dma_start(out=wm_raw[:], in_=wm.rearrange("(p t) e -> p t e", t=PACK))
         ms_raw = sb.tile([P, PACK, M], F32, name="ms_raw")
         nc.sync.dma_start(out=ms_raw[:], in_=mstore.rearrange("(p t) m -> p t m", t=PACK))
+        idx2 = load_list("idx2", offs2)
+        note_planes = load_pairs("notes", notes)
         idx = load_list("idx", offs)
         key_words = sb.tile([P, T], I32, name="key_words")
         nc.sync.dma_start(out=key_words[:], in_=keys_words[0].rearrange("p n t -> p (n t)").bitcast(I32))
-        idx2 = load_list("idx2", offs2)
-        note_planes = load_pairs("notes", notes)
         idx4 = load_list("idx4", offs4)
         idx3 = load_list("idx3", offs3)
         given_planes = load_pairs("given", given)
         val_rows = []
         for e in range(E_TILES):
-            tile = sb.tile([P, T], F32, name="vals%d" % e, tag="vals%d" % e)
+            tile = sb.tile([P, T], F32, name="vals%d" % e, tag="vals%d" % e, align_bytes=64)
             nc.sync.dma_start(out=tile[:], in_=vals[e * P : (e + 1) * P, :])
             val_rows.append(tile)
 
@@ -117,6 +117,13 @@ def tile_attend_tab_timestable_gains_kernel(
                 product(nc, bank[:], wm_q, slice(e * P, (e + 1) * P), ms_q)
                 nc.scalar.copy(out=me[e][:, h * BANK : (h + 1) * BANK], in_=bank[:])
 
+        note_cols = sb.tile([P, PACK, J], F32, name="note_cols")
+        for t in range(PACK):
+            nc.vector.tensor_copy(out=note_cols[:, t, :], in_=note_planes[t].indirect(idx2[:]))
+        note_grouped = sb.tile([P, J, PACK], BF16, name="note_grouped", align_bytes=64)
+        interleave(nc.vector.tensor_copy, note_grouped[:], note_cols[:])
+        note_q = quantize(nc, sb, "notes", note_grouped[:])
+
         key_codes = sb.tile([P, I], U32, name="key_codes", align_bytes=64)
         key_scales = sb.tile([P, I], U8, name="key_scales", align_bytes=64)
         nc.vector.tensor_copy(
@@ -125,13 +132,6 @@ def tile_attend_tab_timestable_gains_kernel(
         nc.vector.tensor_copy(
             out=key_codes[:].rearrange("p (t s) -> p s t", t=PACK), in_=key_words[:].bitcast(U32).indirect(idx[:])
         )
-
-        note_cols = sb.tile([P, PACK, J], F32, name="note_cols")
-        for t in range(PACK):
-            nc.vector.tensor_copy(out=note_cols[:, t, :], in_=note_planes[t].indirect(idx2[:]))
-        note_grouped = sb.tile([P, J, PACK], BF16, name="note_grouped", align_bytes=64)
-        interleave(nc.vector.tensor_copy, note_grouped[:], note_cols[:])
-        note_q = quantize(nc, sb, "notes", note_grouped[:])
 
         me_cols = []
         for e in range(E_TILES):
@@ -159,17 +159,18 @@ def tile_attend_tab_timestable_gains_kernel(
         interleave(nc.vector.tensor_copy, table_grouped[:], table[:])
         table_q = quantize(nc, sb, "table", table_grouped[:])
 
-        half = 288
 
         def turn(e):
             val_cols = sb.tile([P, I], BF16, name="val_cols%d" % e)
-            nc.vector.tensor_copy(out=val_cols[:, :half], in_=val_rows[e][:].indirect(idx[:, : half // 16]))
+            half = 288 if e else 0
+            if half:
+                nc.vector.tensor_copy(out=val_cols[:, :half], in_=val_rows[e][:].indirect(idx[:, : half // 16]))
             nc.scalar.activation(val_cols[:, half:], val_rows[e][:].indirect(idx[:, half // 16 :]), COPY)
             words = val_cols[:].bitcast(F32)
             turned = narrow.tile([P, 2, P], F32, name="turned")
             for u in range(2):
                 nc.tensor.transpose(turned[:, u, :], words[:, u : I // 2 : 2], ident[:])
-            val_grouped = sb.tile([P, P, PACK], BF16, name="val_grouped%d" % e, align_bytes=64)
+            val_grouped = sb.tile([P, P, PACK], BF16, name="val_grouped%d" % e, tag="grouped%d" % e if e else "vals1", align_bytes=64)
             nc.scalar.copy(
                 out=val_grouped[:].rearrange("p c t -> p (c t)").bitcast(F32).rearrange("p (c u) -> p c u", u=2),
                 in_=turned[:].rearrange("p u c -> p c u"),
@@ -177,19 +178,22 @@ def tile_attend_tab_timestable_gains_kernel(
             return val_grouped
 
         def multiply(e, val_grouped):
-            val_q = quantize(nc, sb, "vals%d" % e, val_grouped[:])
+            val_q = quantize(nc, sb, "vals%d" % e, val_grouped[:], tag="vals%d" % (e + 1) if e else None)
             sums = narrow.tile([P, J], F32, name="sums")
             product(nc, sums[:], val_q, slice(0, P), table_q)
             return sums
 
         def finish(e, sums):
-            result = sb.tile([P, J], F32, name="result%d" % e, tag="vals%d" % (e + 1))
+            result = sb.tile([P, J], F32, name="result%d" % e, tag="grouped%d" % (e + 1), align_bytes=64)
             nc.vector.tensor_tensor(out=result[:], in0=sums[:], in1=me_cols[e][:], op=MULT)
             nc.sync.dma_start(out=out[e * P : (e + 1) * P, :], in_=result[:])
 
-        sums = multiply(0, turn(0))
-        for e in range(1, E_TILES):
-            val_grouped = turn(e)
-            finish(e - 1, sums)
-            sums = multiply(e, val_grouped)
-        finish(E_TILES - 1, sums)
+        turned_vals = {0: turn(0)}
+        sums = {}
+        for e in range(E_TILES + 1):
+            if e + 1 < E_TILES:
+                turned_vals[e + 1] = turn(e + 1)
+            if e < E_TILES:
+                sums[e] = multiply(e, turned_vals[e])
+            if e > 0:
+                finish(e - 1, sums[e - 1])

@@ -34,13 +34,13 @@ def quantize(nc, pool, name, grouped, tag=None):
     return codes, scales
 
 
-def product(nc, out, lhs, lhs_cols, rhs):
+def product(nc, out, lhs, lhs_cols, rhs, rhs_cols=slice(None)):
     nc.tensor.matmul_mx(
         out=out,
         lhsT=lhs[0][:, lhs_cols].bitcast(FP8X4),
         lhsT_scale=lhs[1][:, lhs_cols],
-        rhs=rhs[0][:].bitcast(FP8X4),
-        rhs_scale=rhs[1][:],
+        rhs=rhs[0][:, rhs_cols].bitcast(FP8X4),
+        rhs_scale=rhs[1][:, rhs_cols],
         start=True,
         stop=True,
     )
@@ -93,11 +93,8 @@ def tile_attend_tab_timestable_gains_kernel(
         make_identity(nc, ident[:])
         key_bytes = sb.tile([P, T], U8, name="key_bytes")
         nc.vector.memset(key_bytes[:].bitcast(I32), 0)
-        for q in range(4):
-            nc.gpsimd.dma_start(
-                out=key_bytes[32 * q : 32 * q + 4, :].bitcast(I32),
-                in_=keys_scales[0, 4 * q : 4 * q + 4, :].bitcast(I32),
-            )
+        for r in range(4):
+            nc.gpsimd.dma_start(out=key_bytes[r:P:32, :].bitcast(I32), in_=keys_scales[0, r:16:4, :].bitcast(I32))
         row_factor = sb.tile([P, PACK], F32, name="row_factor")
         nc.gpsimd.dma_start(out=row_factor[:], in_=rowf.rearrange("(p t) o -> p (t o)", t=PACK))
 
@@ -177,16 +174,23 @@ def tile_attend_tab_timestable_gains_kernel(
             )
             return val_grouped
 
+        def pieces(e):
+            return [slice(0, J)] if e + 1 < E_TILES else [slice(0, J // 2), slice(J // 2, J)]
+
         def multiply(e, val_grouped):
             val_q = quantize(nc, sb, "vals%d" % e, val_grouped[:], tag="vals%d" % (e + 1) if e else None)
-            sums = narrow.tile([P, J], F32, name="sums")
-            product(nc, sums[:], val_q, slice(0, P), table_q)
+            sums = []
+            for cols in pieces(e):
+                bank = wide.tile([P, cols.stop - cols.start], F32, name="bank")
+                product(nc, bank[:], val_q, slice(0, P), table_q, cols)
+                sums.append(bank)
             return sums
 
         def finish(e, sums):
             result = sb.tile([P, J], F32, name="result%d" % e, tag="grouped%d" % (e + 1), align_bytes=64)
-            nc.vector.tensor_tensor(out=result[:], in0=sums[:], in1=me_cols[e][:], op=MULT)
-            nc.sync.dma_start(out=out[e * P : (e + 1) * P, :], in_=result[:])
+            for cols, bank in zip(pieces(e), sums):
+                nc.vector.tensor_tensor(out=result[:, cols], in0=bank[:], in1=me_cols[e][:, cols], op=MULT)
+                nc.sync.dma_start(out=out[e * P : (e + 1) * P, cols], in_=result[:, cols])
 
         turned_vals = {0: turn(0)}
         sums = {}

from contextlib import ExitStack

import concourse.mybir as mybir
from concourse.masks import make_identity

D, T, I, J, U, Z, E, M, C = 512, 2048, 512, 256, 1024, 1024, 512, 1024, 512
FLOPS = 2 * (D * I * J + I * E * J + C * E * M)

F32 = mybir.dt.float32
BF16 = mybir.dt.bfloat16
I32 = mybir.dt.int32
U32 = mybir.dt.uint32
U16 = mybir.dt.uint16
U8 = mybir.dt.uint8
FP8X4 = mybir.dt.float8_e4m3fn_x4
MULT = mybir.AluOpType.mult
COPY = mybir.ActivationFunctionType.Copy

P = 128
PACK = 4
BANK = 512
E_TILES = E // P


def interleave(copy, dst, src):
    copy(out=dst.rearrange("p (c i) t -> p c t i", i=4), in_=src.rearrange("p t (c i) -> p c t i", i=4))


def quantize(nc, pool, name, grouped, tag=None):
    width = grouped.shape[1]
    codes = pool.tile([P, width], U32, name=name + "_codes", tag=tag or name + "_codes", align_bytes=64)
    scales = pool.tile([P, width], U8, name=name + "_scales", align_bytes=64)
    nc.vector.quantize_mx(out=codes[:].bitcast(FP8X4), scales=scales[:], in_=grouped.rearrange("p c t -> p (c t)"))
    return codes, scales


def product(nc, out, lhs, lhs_cols, rhs, rhs_cols=slice(None)):
    nc.tensor.matmul_mx(
        out=out,
        lhsT=lhs[0][:, lhs_cols].bitcast(FP8X4),
        lhsT_scale=lhs[1][:, lhs_cols],
        rhs=rhs[0][:, rhs_cols].bitcast(FP8X4),
        rhs_scale=rhs[1][:, rhs_cols],
        start=True,
        stop=True,
    )


def tile_attend_tab_timestable_gains_kernel(
    tc, keys_words, keys_scales, notes, given, rowf, vals, wm, mstore, offs, offs2, offs3, offs4, out
):
    nc = tc.nc
    with ExitStack() as ctx:
        lists = ctx.enter_context(tc.tile_pool(name="lists", bufs=1))
        sb = ctx.enter_context(tc.tile_pool(name="sb", bufs=1))
        wide = ctx.enter_context(tc.psum_pool(name="wide", bufs=4))
        narrow = ctx.enter_context(tc.psum_pool(name="narrow", bufs=2))

        def load_list(name, src):
            tile = lists.tile(list(src.shape), U16, name=name)
            nc.sync.dma_start(tile[:], src)
            return tile

        def load_pairs(name, src):
            width = src.shape[1]
            rows = src.rearrange("(p t) w -> p t w", t=PACK)
            planes = []
            for h in range(2):
                tile = sb.tile([P, 2, width], F32, name="%s%d" % (name, h))
                nc.sync.dma_start(out=tile[:], in_=rows[:, 2 * h : 2 * h + 2, :])
                planes += [tile[:, 0, :], tile[:, 1, :]]
            return planes

        wm_raw = sb.tile([P, PACK, E], F32, name="wm_raw")
        nc.sync.dma_start(out=wm_raw[:], in_=wm.rearrange("(p t) e -> p t e", t=PACK))
        ms_raw = sb.tile([P, PACK, M], F32, name="ms_raw")
        nc.sync.dma_start(out=ms_raw[:], in_=mstore.rearrange("(p t) m -> p t m", t=PACK))
        idx2 = load_list("idx2", offs2)
        note_planes = load_pairs("notes", notes)
        idx = load_list("idx", offs)
        key_words = sb.tile([P, T], I32, name="key_words")
        nc.sync.dma_start(out=key_words[:], in_=keys_words[0].rearrange("p n t -> p (n t)").bitcast(I32))
        idx4 = load_list("idx4", offs4)
        idx3 = load_list("idx3", offs3)
        given_planes = load_pairs("given", given)
        val_rows = []
        for e in range(E_TILES):
            tile = sb.tile([P, T], F32, name="vals%d" % e, tag="vals%d" % e, align_bytes=64)
            nc.sync.dma_start(out=tile[:], in_=vals[e * P : (e + 1) * P, :])
            val_rows.append(tile)

        ident = sb.tile([P, P], F32, name="ident")
        make_identity(nc, ident[:])
        key_bytes = sb.tile([P, T], U8, name="key_bytes")
        nc.vector.memset(key_bytes[:].bitcast(I32), 0)
        for r in range(4):
            nc.gpsimd.dma_start(out=key_bytes[r:P:32, :].bitcast(I32), in_=keys_scales[0, r:16:4, :].bitcast(I32))
        row_factor = sb.tile([P, PACK], F32, name="row_factor")
        nc.gpsimd.dma_start(out=row_factor[:], in_=rowf.rearrange("(p t) o -> p (t o)", t=PACK))

        wm_grouped = sb.tile([P, E, PACK], BF16, name="wm_grouped", align_bytes=64)
        interleave(nc.vector.tensor_copy, wm_grouped[:], wm_raw[:])
        wm_q = quantize(nc, sb, "wm", wm_grouped[:])
        ms_grouped = []
        for h, copy in enumerate((nc.vector.tensor_copy, nc.scalar.copy)):
            grouped = sb.tile([P, BANK, PACK], BF16, name="ms_grouped%d" % h, align_bytes=64)
            interleave(copy, grouped[:], ms_raw[:, :, h * BANK : (h + 1) * BANK])
            ms_grouped.append(grouped)
        me = [sb.tile([P, M], F32, name="me%d" % e) for e in range(E_TILES)]
        for h in range(2):
            ms_q = quantize(nc, sb, "ms%d" % h, ms_grouped[h][:])
            for e in range(E_TILES):
                bank = wide.tile([P, BANK], F32, name="bank")
                product(nc, bank[:], wm_q, slice(e * P, (e + 1) * P), ms_q)
                nc.scalar.copy(out=me[e][:, h * BANK : (h + 1) * BANK], in_=bank[:])

        note_cols = sb.tile([P, PACK, J], F32, name="note_cols")
        for t in range(PACK):
            nc.vector.tensor_copy(out=note_cols[:, t, :], in_=note_planes[t].indirect(idx2[:]))
        note_grouped = sb.tile([P, J, PACK], BF16, name="note_grouped", align_bytes=64)
        interleave(nc.vector.tensor_copy, note_grouped[:], note_cols[:])
        note_q = quantize(nc, sb, "notes", note_grouped[:])

        key_codes = sb.tile([P, I], U32, name="key_codes", align_bytes=64)
        key_scales = sb.tile([P, I], U8, name="key_scales", align_bytes=64)
        nc.vector.tensor_copy(
            out=key_scales[:].rearrange("p (t s) -> p s t", t=PACK), in_=key_bytes[:].indirect(idx[:])
        )
        nc.vector.tensor_copy(
            out=key_codes[:].rearrange("p (t s) -> p s t", t=PACK), in_=key_words[:].bitcast(U32).indirect(idx[:])
        )

        me_cols = []
        for e in range(E_TILES):
            cols = sb.tile([P, J], F32, name="me_cols%d" % e)
            nc.scalar.activation(cols[:], me[e][:].indirect(idx4[:]), COPY)
            me_cols.append(cols)

        table = sb.tile([P, PACK, J], BF16, name="table")
        for h in range(2):
            bank = wide.tile([P, BANK], F32, name="bank")
            for t in (2 * h, 2 * h + 1):
                product(nc, bank[:, (t % 2) * J : (t % 2 + 1) * J], (key_codes, key_scales), slice(t * P, (t + 1) * P), note_q)
            for t in (2 * h, 2 * h + 1):
                given_cols = sb.tile([P, J], F32, name="given_cols%d" % t)
                nc.scalar.activation(given_cols[:], given_planes[t].indirect(idx3[:]), COPY)
                nc.vector.scalar_tensor_tensor(
                    out=table[:, t, :],
                    in0=given_cols[:],
                    scalar=row_factor[:, t : t + 1],
                    in1=bank[:, (t % 2) * J : (t % 2 + 1) * J],
                    op0=MULT,
                    op1=MULT,
                )
        table_grouped = sb.tile([P, J, PACK], BF16, name="table_grouped", align_bytes=64)
        interleave(nc.vector.tensor_copy, table_grouped[:], table[:])
        table_q = quantize(nc, sb, "table", table_grouped[:])


        def turn(e):
            val_cols = sb.tile([P, I], BF16, name="val_cols%d" % e)
            half = 288 if e else 0
            if half:
                nc.vector.tensor_copy(out=val_cols[:, :half], in_=val_rows[e][:].indirect(idx[:, : half // 16]))
            nc.scalar.activation(val_cols[:, half:], val_rows[e][:].indirect(idx[:, half // 16 :]), COPY)
            words = val_cols[:].bitcast(F32)
            turned = narrow.tile([P, 2, P], F32, name="turned")
            for u in range(2):
                nc.tensor.transpose(turned[:, u, :], words[:, u : I // 2 : 2], ident[:])
            val_grouped = sb.tile([P, P, PACK], BF16, name="val_grouped%d" % e, tag="grouped%d" % e if e else "vals1", align_bytes=64)
            nc.scalar.copy(
                out=val_grouped[:].rearrange("p c t -> p (c t)").bitcast(F32).rearrange("p (c u) -> p c u", u=2),
                in_=turned[:].rearrange("p u c -> p c u"),
            )
            return val_grouped

        def pieces(e):
            return [slice(0, J)] if e + 1 < E_TILES else [slice(0, J // 2), slice(J // 2, J)]

        def multiply(e, val_grouped):
            val_q = quantize(nc, sb, "vals%d" % e, val_grouped[:], tag="vals%d" % (e + 1) if e else None)
            sums = []
            for cols in pieces(e):
                bank = wide.tile([P, cols.stop - cols.start], F32, name="bank")
                product(nc, bank[:], val_q, slice(0, P), table_q, cols)
                sums.append(bank)
            return sums

        def finish(e, sums):
            result = sb.tile([P, J], F32, name="result%d" % e, tag="grouped%d" % (e + 1), align_bytes=64)
            for cols, bank in zip(pieces(e), sums):
                nc.vector.tensor_tensor(out=result[:, cols], in0=bank[:], in1=me_cols[e][:, cols], op=MULT)
                nc.sync.dma_start(out=out[e * P : (e + 1) * P, cols], in_=result[:, cols])

        turned_vals = {0: turn(0)}
        sums = {}
        for e in range(E_TILES + 1):
            if e + 1 < E_TILES:
                turned_vals[e + 1] = turn(e + 1)
            if e < E_TILES:
                sums[e] = multiply(e, turned_vals[e])
            if e > 0:
                finish(e - 1, sums[e - 1])
